import numpy as np
import ml_dtypes


def mxq(x, axis, fmt="e4m3"):
    dtype, down = {"e4m3": (ml_dtypes.float8_e4m3fn, 7), "e5m2": (ml_dtypes.float8_e5m2, 14)}[fmt]
    v = np.moveaxis(np.asarray(x, np.float32).astype(ml_dtypes.bfloat16).astype(np.float64), axis, -1)
    blocks = v.reshape(v.shape[:-1] + (-1, 32))
    amax = np.abs(blocks).max(-1, keepdims=True)
    byte = np.maximum(np.where(amax > 0, np.frexp(amax)[1] - 1 + 127, 0) - down, 1)
    scale = np.exp2(byte - 127.0)
    codes = (blocks / scale).astype(np.float32).astype(dtype).astype(np.float64)
    return np.moveaxis((codes * scale).reshape(v.shape), -1, axis)


WIDE = False


def mx_kscale(k):
    if not WIDE:
        return np.ones(k)
    levels = np.array([10, -10, 5, -5, 0])
    if k % 512:
        return np.exp2(np.random.permutation(np.resize(levels, k // 32))).repeat(32)
    a = np.empty((k // 512, 16))
    for p in range(k // 512):
        a[p, :8] = np.random.permutation(np.resize(levels, 8))
        for g in range(8):
            far = levels[np.abs(levels - a[p, g]) >= 10]
            a[p, g + 8] = far[np.random.randint(len(far))]
    return np.exp2(a.ravel()).repeat(32)


BF16 = ml_dtypes.bfloat16


def bf(x):
    return np.asarray(x, np.float32).astype(BF16)


def f64(x):
    return np.asarray(x).astype(np.float64)

def planes(Y):
    n, m = Y.shape
    b = f64(bf(Y)).reshape(n // 32, 32, m)
    amax = np.abs(b).max(1)
    byte = np.clip(np.where(amax > 0, np.frexp(amax)[1] - 1 + 127 - 7, 1), 1, 254)
    codes = (b * np.exp2(127.0 - byte)[:, None, :]).reshape(n, m).astype(np.float32).astype(ml_dtypes.float8_e4m3fn).view(np.uint8)
    words = codes.reshape(n // 512, 128, 4, m).transpose(0, 1, 3, 2)
    return np.ascontiguousarray(words), np.ascontiguousarray(byte.astype(np.uint8).reshape(n // 512, 16, m))


B, C, S, F = 16, 1024, 256, 512


def setup_inputs():
    k = mx_kscale(C)
    chan_amp = np.exp(0.4 * np.random.randn(C))
    trial_amp = np.exp(0.3 * np.random.randn(B))
    x = np.random.randn(B, C, S) * chan_amp[None, :, None] * trial_amp[:, None, None]
    w = np.random.randn(C, F) / np.sqrt(C) * np.exp(0.3 * np.random.randn(F))[None, :]
    power_offset = 0.3 * np.exp(0.3 * np.random.randn(F))
    gain = np.exp(0.8 * np.random.randn(F))
    return {
        "x": bf(x * k[None, :, None]),
        "w": bf(w / k[:, None]),
        "power_offset": bf(power_offset),
        "gain": bf(gain),
    }

def reference(x, w, power_offset, gain):
    xq = mxq(f64(x), 1, "e4m3").transpose(1, 0, 2).reshape(C, B * S)
    wq = mxq(f64(w), 0, "e4m3")
    z = (wq.T @ xq).reshape(F, B, S).transpose(1, 0, 2)
    y = np.log(np.square(z) + f64(power_offset)[None, :, None]) * f64(gain)[None, :, None]
    Y = y.transpose(1, 0, 2).reshape(F, B * S)
    words, scales = planes(Y)
    return y, words, scales

@@ -1,0 +1,237 @@
+from contextlib import ExitStack
+
+import concourse.mybir as mybir
+
+B, C, S, F = 16, 1024, 256, 512
+FLOPS = 2 * B * C * S * F
+
+F32 = mybir.dt.float32
+BF16 = mybir.dt.bfloat16
+I32 = mybir.dt.int32
+U32 = mybir.dt.uint32
+U8 = mybir.dt.uint8
+FP8X4 = mybir.dt.float8_e4m3fn_x4
+ACT = mybir.ActivationFunctionType
+ALU = mybir.AluOpType
+
+P = 128
+PACK = 4
+K_PASS = P * PACK
+PASSES = C // K_PASS
+RUN = 4
+TILES = [[0]] + [[b, b + 1] for b in range(1, B - 1, 2)] + [[B - 1]]
+LEAD = 2
+SCALAR_UNITS = [(1, 0), (2, 0), (4, 0), (6, 0), (8, 0), (9, 0), (11, 0), (12, 0), (13, 0)]
+
+
+def tile_eeg_log_power_planes_g2_kernel(tc, x, w, power_offset, gain, out_0, out_1, out_2):
+    nc = tc.nc
+    n_tiles = len(TILES)
+    words_hbm = out_1[0].rearrange("p m t -> p (m t)").bitcast(I32)
+    scales_hbm = out_2[0].bitcast(I32)
+
+    with ExitStack() as ctx:
+        keep = ctx.enter_context(tc.tile_pool(name="keep", bufs=1))
+        xg_pool = ctx.enter_context(tc.tile_pool(name="xg", bufs=3))
+        xq_pool = ctx.enter_context(tc.tile_pool(name="xq", bufs=4))
+        sq_pool = ctx.enter_context(tc.tile_pool(name="sq", bufs=4))
+        lg_pool = ctx.enter_context(tc.tile_pool(name="lg", bufs=8))
+        y_pool = ctx.enter_context(tc.tile_pool(name="y", bufs=4))
+        yb_pool = ctx.enter_context(tc.tile_pool(name="yb", bufs=2))
+        psum = ctx.enter_context(tc.psum_pool(name="psum", bufs=8))
+        ctx.enter_context(tc.manual_schedule())
+
+        off_bf = keep.tile([P, PACK], BF16, name="off_bf")
+        gain_bf = keep.tile([P, PACK], BF16, name="gain_bf")
+        off = keep.tile([P, PACK], F32, name="off")
+        gn = keep.tile([P, PACK], F32, name="gn")
+        w_raw = [keep.tile([P, PACK, F], BF16, name="w_raw%d" % g) for g in range(PASSES)]
+        w_grouped = [keep.tile([P, F * PACK], BF16, name="w_grouped%d" % g, align_bytes=64) for g in range(PASSES)]
+        w_codes = [keep.tile([P, F], U32, name="w_codes%d" % g, align_bytes=64) for g in range(PASSES)]
+        w_scales = [keep.tile([P, F], U8, name="w_scales%d" % g, align_bytes=64) for g in range(PASSES)]
+        x_raw = [keep.tile([P, PASSES, PACK, S], BF16, name="x_raw%d" % b) for b in range(B)]
+        y_words = keep.tile([P, B * S], U32, name="y_words", align_bytes=64)
+        y_scales = keep.tile([P, B * S], U8, name="y_scales", align_bytes=64)
+
+        def load_w(g):
+            nc.sync.dma_start(out=w_raw[g][:], in_=w[g * K_PASS : (g + 1) * K_PASS, :].rearrange("(p j) f -> p j f", j=PACK))
+
+        def x_view(b):
+            return x[b].rearrange("(g p j) s -> p g j s", g=PASSES, j=PACK)
+
+        nc.scalar.dma_start(out=off_bf[:], in_=power_offset.rearrange("(p t) -> p t", t=PACK))
+        nc.scalar.dma_start(out=gain_bf[:], in_=gain.rearrange("(p t) -> p t", t=PACK))
+        nc.scalar.copy(out=off[:], in_=off_bf[:])
+        nc.scalar.copy(out=gn[:], in_=gain_bf[:])
+        for g in range(PASSES):
+            load_w(g)
+            nc.sync.dma_start(out=x_raw[0][:, g], in_=x_view(0)[:, g])
+        for b in range(1, B):
+            nc.sync.dma_start(out=x_raw[b][:], in_=x_view(b))
+
+        x_grouped, x_codes, x_scales, banks, squares, logs, ys, ybs = {}, {}, {}, {}, {}, {}, {}, {}
+
+        def width(i):
+            return len(TILES[i]) * S
+
+        def copy_on(on_scalar, out, in_):
+            if on_scalar:
+                nc.scalar.copy(out=out, in_=in_)
+            else:
+                nc.vector.tensor_copy(out=out, in_=in_)
+
+        def interleave_w(g, half, on_scalar):
+            ts = slice(2 * half, 2 * half + 2)
+            dst = w_grouped[g][:].rearrange("p (t m j) -> p t m j", t=PACK, j=PACK)[:, ts]
+            src = w_raw[g][:].rearrange("p j (m t) -> p t m j", t=PACK)[:, ts]
+            copy_on(on_scalar, dst, src)
+
+        def quantize_w(g):
+            nc.vector.quantize_mx(out=w_codes[g][:].bitcast(FP8X4), scales=w_scales[g][:], in_=w_grouped[g][:])
+
+        def open_x(i):
+            x_grouped[i] = xg_pool.tile([P, PASSES, 2 * S * PACK], BF16, name="x_grouped", align_bytes=64)
+            x_codes[i] = xq_pool.tile([P, PASSES, 2 * S], U32, name="x_codes", align_bytes=64)
+            x_scales[i] = xq_pool.tile([P, PASSES, 2 * S], U8, name="x_scales", align_bytes=64)
+
+        def interleave_x(i, b, gs, on_scalar):
+            at = TILES[i].index(b) * S * PACK
+            dst = x_grouped[i][:, gs, at : at + S * PACK].rearrange("p g (c r j) -> p g c j r", r=RUN, j=PACK)
+            src = x_raw[b][:, gs].rearrange("p g j (c r) -> p g c j r", r=RUN)
+            copy_on(on_scalar, dst, src)
+
+        def quantize_x(i, g):
+            n = width(i)
+            nc.vector.quantize_mx(
+                out=x_codes[i][:, g, :n].bitcast(FP8X4), scales=x_scales[i][:, g, :n], in_=x_grouped[i][:, g, : n * PACK]
+            )
+
+        def multiply(i):
+            n = width(i)
+            for t in range(PACK):
+                bank = psum.tile([P, 2 * S], F32, name="bank")
+                banks[i, t] = bank
+                cols = slice(t * P, (t + 1) * P)
+                for g in range(PASSES):
+                    nc.tensor.matmul_mx(
+                        out=bank[:, :n],
+                        lhsT=w_codes[g][:, cols].bitcast(FP8X4),
+                        lhsT_scale=w_scales[g][:, cols],
+                        rhs=x_codes[i][:, g, :n].bitcast(FP8X4),
+                        rhs_scale=x_scales[i][:, g, :n],
+                        start=(g == 0),
+                        stop=(g == PASSES - 1),
+                    )
+
+        def square(i, t):
+            n = width(i)
+            squares[i, t] = sq_pool.tile([P, 2 * S], F32, name="square")
+            nc.scalar.activation(out=squares[i, t][:, :n], in_=banks[i, t][:, :n], func=ACT.Square)
+
+        def log(i, t):
+            n = width(i)
+            logs[i, t] = lg_pool.tile([P, 2 * S], F32, name="logp")
+            nc.scalar.activation(out=logs[i, t][:, :n], in_=squares[i, t][:, :n], func=ACT.Ln, bias=off[:, t : t + 1])
+
+        def apply_gain(i):
+            nb = len(TILES[i])
+            ys[i] = y_pool.tile([P, 2, PACK, S], F32, name="y")
+            for t in range(PACK):
+                nc.vector.tensor_scalar(
+                    out=ys[i][:, :nb, t, :],
+                    in0=logs[i, t][:, : nb * S].rearrange("p (b s) -> p b s", s=S),
+                    scalar1=gn[:, t : t + 1],
+                    scalar2=None,
+                    op0=ALU.mult,
+                )
+            b0 = TILES[i][0]
+            nc.sync.dma_start(
+                out=out_0[b0 : b0 + nb].rearrange("b (p t) s -> p b t s", t=PACK), in_=ys[i][:, :nb]
+            )
+
+        def round_y(i):
+            nb = len(TILES[i])
+            ybs[i] = yb_pool.tile([P, 2 * S * PACK], BF16, name="y_bf", align_bytes=64)
+            dst = ybs[i][:, : nb * S * PACK].rearrange("p (b c r t) -> p b c t r", b=nb, r=RUN, t=PACK)
+            src = ys[i][:, :nb].rearrange("p b t (c r) -> p b c t r", r=RUN)
+            nc.vector.tensor_copy(out=dst, in_=src)
+
+        def quantize_y(i):
+            n = width(i)
+            cols = slice(TILES[i][0] * S, TILES[i][0] * S + n)
+            nc.vector.quantize_mx(out=y_words[:, cols].bitcast(FP8X4), scales=y_scales[:, cols], in_=ybs[i][:, : n * PACK])
+            nc.sync.dma_start(out=words_hbm[:, cols], in_=y_words[:, cols].bitcast(I32))
+
+        def store_scales(first, last):
+            cols = slice(first // PACK, last // PACK)
+            for q in range(4):
+                nc.sync.dma_start(
+                    out=scales_hbm[4 * q : 4 * q + 4, cols], in_=y_scales[:].bitcast(I32)[32 * q : 32 * q + 4, cols]
+                )
+
+        def vector_units(i):
+            units = []
+            for b in TILES[i]:
+                first = 1 if (b, 0) in SCALAR_UNITS else 0
+                units.append((b, slice(first, PASSES)))
+            return units
+
+        def scalar_interleaves(i):
+            for b in TILES[i]:
+                if (b, 0) in SCALAR_UNITS:
+                    interleave_x(i, b, slice(0, 1), True)
+
+        open_x(0)
+        interleave_w(0, 0, False)
+        interleave_w(0, 1, True)
+        interleave_x(0, 0, slice(0, 1), False)
+        interleave_w(1, 0, False)
+        interleave_w(1, 1, True)
+        quantize_w(0)
+        interleave_x(0, 0, slice(1, 2), False)
+        quantize_x(0, 0)
+        quantize_w(1)
+        quantize_x(0, 1)
+        multiply(0)
+        open_x(1)
+        scalar_interleaves(1)
+        for b, gs in vector_units(1):
+            interleave_x(1, b, gs, False)
+        quantize_x(1, 0)
+        quantize_x(1, 1)
+        multiply(1)
+
+        for j in range(n_tiles + 1):
+            ahead = j + LEAD
+            units = vector_units(ahead) if ahead < n_tiles else []
+            if j < n_tiles:
+                square(j, 0)
+                square(j, 1)
+                log(j, 0)
+                log(j, 1)
+            if ahead < n_tiles:
+                open_x(ahead)
+                scalar_interleaves(ahead)
+            if j < n_tiles:
+                square(j, 2)
+                square(j, 3)
+                log(j, 2)
+                log(j, 3)
+            if j >= 1:
+                apply_gain(j - 1)
+            for b, gs in units[:1]:
+                interleave_x(ahead, b, gs, False)
+            if j >= 1:
+                round_y(j - 1)
+            for b, gs in units[1:]:
+                interleave_x(ahead, b, gs, False)
+            if ahead < n_tiles:
+                quantize_x(ahead, 0)
+            if j >= 1:
+                quantize_y(j - 1)
+            if ahead < n_tiles:
+                quantize_x(ahead, 1)
+                multiply(ahead)
+            if j == n_tiles - 1:
+                store_scales(0, (B - 1) * S)
+        store_scales((B - 1) * S, B * S)

@@ -21,7 +21,10 @@ PASSES = C // K_PASS
 RUN = 4
 TILES = [[0]] + [[b, b + 1] for b in range(1, B - 1, 2)] + [[B - 1]]
 LEAD = 2
-SCALAR_UNITS = [(1, 0), (2, 0), (4, 0), (6, 0), (8, 0), (9, 0), (11, 0), (12, 0), (13, 0)]
+SCALAR_UNITS = [(b, 0) for b in (1, 2, 3, 5, 7, 9, 11, 13)]
+PAIR = 2
+SCALAR_SAMPLES = {len(TILES) - 2: 64, len(TILES) - 1: 96}
+SCALE_STORES = (2, 5)
 
 
 def tile_eeg_log_power_planes_g2_kernel(tc, x, w, power_offset, gain, out_0, out_1, out_2):
@@ -36,7 +39,7 @@ def tile_eeg_log_power_planes_g2_kernel(tc, x, w, power_offset, gain, out_0, out
         xq_pool = ctx.enter_context(tc.tile_pool(name="xq", bufs=4))
         sq_pool = ctx.enter_context(tc.tile_pool(name="sq", bufs=4))
         lg_pool = ctx.enter_context(tc.tile_pool(name="lg", bufs=8))
-        y_pool = ctx.enter_context(tc.tile_pool(name="y", bufs=4))
+        y_pool = ctx.enter_context(tc.tile_pool(name="y", bufs=6))
         yb_pool = ctx.enter_context(tc.tile_pool(name="yb", bufs=2))
         psum = ctx.enter_context(tc.psum_pool(name="psum", bufs=8))
         ctx.enter_context(tc.manual_schedule())
@@ -81,62 +84,73 @@ def tile_eeg_log_power_planes_g2_kernel(tc, x, w, power_offset, gain, out_0, out
                 nc.vector.tensor_copy(out=out, in_=in_)
 
         def interleave_w(g, half, on_scalar):
-            ts = slice(2 * half, 2 * half + 2)
-            dst = w_grouped[g][:].rearrange("p (t m j) -> p t m j", t=PACK, j=PACK)[:, ts]
-            src = w_raw[g][:].rearrange("p j (m t) -> p t m j", t=PACK)[:, ts]
+            ms = slice(32 * half, 32 * half + 32)
+            dst = w_grouped[g][:].rearrange("p (t m e j) -> p m t j e", t=PACK, e=PAIR, j=PACK)[:, ms]
+            src = w_raw[g][:].rearrange("p j (m e t) -> p m t j e", t=PACK, e=PAIR)[:, ms]
             copy_on(on_scalar, dst, src)
 
         def quantize_w(g):
             nc.vector.quantize_mx(out=w_codes[g][:].bitcast(FP8X4), scales=w_scales[g][:], in_=w_grouped[g][:])
 
         def open_x(i):
-            x_grouped[i] = xg_pool.tile([P, PASSES, 2 * S * PACK], BF16, name="x_grouped", align_bytes=64)
-            x_codes[i] = xq_pool.tile([P, PASSES, 2 * S], U32, name="x_codes", align_bytes=64)
-            x_scales[i] = xq_pool.tile([P, PASSES, 2 * S], U8, name="x_scales", align_bytes=64)
+            x_grouped[i] = xg_pool.tile([P, PASSES * 2 * S * PACK], BF16, name="x_grouped", align_bytes=64)
+            x_codes[i] = xq_pool.tile([P, PASSES * 2 * S], U32, name="x_codes", align_bytes=64)
+            x_scales[i] = xq_pool.tile([P, PASSES * 2 * S], U8, name="x_scales", align_bytes=64)
 
         def interleave_x(i, b, gs, on_scalar):
             at = TILES[i].index(b) * S * PACK
-            dst = x_grouped[i][:, gs, at : at + S * PACK].rearrange("p g (c r j) -> p g c j r", r=RUN, j=PACK)
+            by_pass = x_grouped[i][:, : PASSES * width(i) * PACK].rearrange("p (g e) -> p g e", g=PASSES)
+            dst = by_pass[:, gs, at : at + S * PACK].rearrange("p g (c r j) -> p g c j r", r=RUN, j=PACK)
             src = x_raw[b][:, gs].rearrange("p g j (c r) -> p g c j r", r=RUN)
             copy_on(on_scalar, dst, src)
 
-        def quantize_x(i, g):
+        def quantize_x(i, gs):
             n = width(i)
+            cols = slice(gs.start * n, gs.stop * n)
             nc.vector.quantize_mx(
-                out=x_codes[i][:, g, :n].bitcast(FP8X4), scales=x_scales[i][:, g, :n], in_=x_grouped[i][:, g, : n * PACK]
+                out=x_codes[i][:, cols].bitcast(FP8X4),
+                scales=x_scales[i][:, cols],
+                in_=x_grouped[i][:, cols.start * PACK : cols.stop * PACK],
             )
 
         def multiply(i):
             n = width(i)
+            per_bank = 2 * S // n
             for t in range(PACK):
-                bank = psum.tile([P, 2 * S], F32, name="bank")
-                banks[i, t] = bank
+                if t % per_bank == 0:
+                    bank = psum.tile([P, 2 * S], F32, name="bank")
+                    banks[i, t // per_bank] = bank
+                at = (t % per_bank) * n
                 cols = slice(t * P, (t + 1) * P)
                 for g in range(PASSES):
                     nc.tensor.matmul_mx(
-                        out=bank[:, :n],
+                        out=bank[:, at : at + n],
                         lhsT=w_codes[g][:, cols].bitcast(FP8X4),
                         lhsT_scale=w_scales[g][:, cols],
-                        rhs=x_codes[i][:, g, :n].bitcast(FP8X4),
-                        rhs_scale=x_scales[i][:, g, :n],
+                        rhs=x_codes[i][:, g * n : (g + 1) * n].bitcast(FP8X4),
+                        rhs_scale=x_scales[i][:, g * n : (g + 1) * n],
                         start=(g == 0),
                         stop=(g == PASSES - 1),
                     )
 
-        def square(i, t):
-            n = width(i)
-            squares[i, t] = sq_pool.tile([P, 2 * S], F32, name="square")
-            nc.scalar.activation(out=squares[i, t][:, :n], in_=banks[i, t][:, :n], func=ACT.Square)
+        def square(i, k):
+            squares[i, k] = sq_pool.tile([P, 2 * S], F32, name="square")
+            nc.scalar.activation(out=squares[i, k][:], in_=banks[i, k][:], func=ACT.Square)
 
         def log(i, t):
             n = width(i)
+            per_bank = 2 * S // n
+            at = (t % per_bank) * n
             logs[i, t] = lg_pool.tile([P, 2 * S], F32, name="logp")
-            nc.scalar.activation(out=logs[i, t][:, :n], in_=squares[i, t][:, :n], func=ACT.Ln, bias=off[:, t : t + 1])
+            nc.scalar.activation(
+                out=logs[i, t][:, :n], in_=squares[i, t // per_bank][:, at : at + n], func=ACT.Ln, bias=off[:, t : t + 1]
+            )
 
-        def apply_gain(i):
+        def apply_gain(i, ts):
             nb = len(TILES[i])
-            ys[i] = y_pool.tile([P, 2, PACK, S], F32, name="y")
-            for t in range(PACK):
+            if ts[0] == 0:
+                ys[i] = y_pool.tile([P, 2, PACK, S], F32, name="y")
+            for t in ts:
                 nc.vector.tensor_scalar(
                     out=ys[i][:, :nb, t, :],
                     in0=logs[i, t][:, : nb * S].rearrange("p (b s) -> p b s", s=S),
@@ -144,17 +158,21 @@ def tile_eeg_log_power_planes_g2_kernel(tc, x, w, power_offset, gain, out_0, out
                     scalar2=None,
                     op0=ALU.mult,
                 )
-            b0 = TILES[i][0]
-            nc.sync.dma_start(
-                out=out_0[b0 : b0 + nb].rearrange("b (p t) s -> p b t s", t=PACK), in_=ys[i][:, :nb]
-            )
+            if ts[-1] == PACK - 1:
+                b0 = TILES[i][0]
+                nc.sync.dma_start(
+                    out=out_0[b0 : b0 + nb].rearrange("b (p t) s -> p b t s", t=PACK), in_=ys[i][:, :nb]
+                )
 
         def round_y(i):
             nb = len(TILES[i])
             ybs[i] = yb_pool.tile([P, 2 * S * PACK], BF16, name="y_bf", align_bytes=64)
-            dst = ybs[i][:, : nb * S * PACK].rearrange("p (b c r t) -> p b c t r", b=nb, r=RUN, t=PACK)
-            src = ys[i][:, :nb].rearrange("p b t (c r) -> p b c t r", r=RUN)
-            nc.vector.tensor_copy(out=dst, in_=src)
+            dst = ybs[i][:, : nb * S * PACK].rearrange("p (b c r t) -> p b c t r", b=nb, r=PAIR, t=PACK)
+            src = ys[i][:, :nb].rearrange("p b t (c r) -> p b c t r", r=PAIR)
+            cut = (S - SCALAR_SAMPLES.get(i, 0)) // PAIR
+            nc.vector.tensor_copy(out=dst[:, :, :cut], in_=src[:, :, :cut])
+            if i in SCALAR_SAMPLES:
+                nc.scalar.copy(out=dst[:, :, cut:], in_=src[:, :, cut:])
 
         def quantize_y(i):
             n = width(i)
@@ -162,10 +180,10 @@ def tile_eeg_log_power_planes_g2_kernel(tc, x, w, power_offset, gain, out_0, out
             nc.vector.quantize_mx(out=y_words[:, cols].bitcast(FP8X4), scales=y_scales[:, cols], in_=ybs[i][:, : n * PACK])
             nc.sync.dma_start(out=words_hbm[:, cols], in_=y_words[:, cols].bitcast(I32))
 
-        def store_scales(first, last):
+        def store_scales(first, last, queues):
             cols = slice(first // PACK, last // PACK)
             for q in range(4):
-                nc.sync.dma_start(
+                queues[q].dma_start(
                     out=scales_hbm[4 * q : 4 * q + 4, cols], in_=y_scales[:].bitcast(I32)[32 * q : 32 * q + 4, cols]
                 )
 
@@ -181,57 +199,72 @@ def tile_eeg_log_power_planes_g2_kernel(tc, x, w, power_offset, gain, out_0, out
                 if (b, 0) in SCALAR_UNITS:
                     interleave_x(i, b, slice(0, 1), True)
 
+        both = slice(0, PASSES)
         open_x(0)
         interleave_w(0, 0, False)
         interleave_w(0, 1, True)
         interleave_x(0, 0, slice(0, 1), False)
+        quantize_w(0)
         interleave_w(1, 0, False)
         interleave_w(1, 1, True)
-        quantize_w(0)
+        quantize_x(0, slice(0, 1))
         interleave_x(0, 0, slice(1, 2), False)
-        quantize_x(0, 0)
         quantize_w(1)
-        quantize_x(0, 1)
+        quantize_x(0, slice(1, 2))
         multiply(0)
         open_x(1)
         scalar_interleaves(1)
         for b, gs in vector_units(1):
             interleave_x(1, b, gs, False)
-        quantize_x(1, 0)
-        quantize_x(1, 1)
-        multiply(1)
 
-        for j in range(n_tiles + 1):
+        open_x(2)
+        square(0, 0)
+        square(0, 1)
+        scalar_interleaves(2)
+        for t in range(PACK):
+            log(0, t)
+        units = vector_units(2)
+        interleave_x(2, units[0][0], units[0][1], False)
+        quantize_x(1, both)
+        multiply(1)
+        interleave_x(2, units[1][0], units[1][1], False)
+
+        stored = 0
+        for j in range(1, n_tiles + 1):
             ahead = j + LEAD
-            units = vector_units(ahead) if ahead < n_tiles else []
-            if j < n_tiles:
-                square(j, 0)
-                square(j, 1)
-                log(j, 0)
-                log(j, 1)
+            done = j - 1
             if ahead < n_tiles:
                 open_x(ahead)
                 scalar_interleaves(ahead)
             if j < n_tiles:
-                square(j, 2)
-                square(j, 3)
-                log(j, 2)
-                log(j, 3)
-            if j >= 1:
-                apply_gain(j - 1)
-            for b, gs in units[:1]:
-                interleave_x(ahead, b, gs, False)
-            if j >= 1:
-                round_y(j - 1)
-            for b, gs in units[1:]:
-                interleave_x(ahead, b, gs, False)
+                if len(TILES[j]) == 2:
+                    for pair in ((0, 1), (2, 3)):
+                        for t in pair:
+                            square(j, t)
+                        for t in pair:
+                            log(j, t)
+                else:
+                    square(j, 0)
+                    square(j, 1)
+                    for t in range(PACK):
+                        log(j, t)
+            if j == 1:
+                apply_gain(done, (0, 1))
+                quantize_x(2, both)
+                multiply(2)
             if ahead < n_tiles:
-                quantize_x(ahead, 0)
-            if j >= 1:
-                quantize_y(j - 1)
+                for b, gs in vector_units(ahead):
+                    interleave_x(ahead, b, gs, False)
+            apply_gain(done, (0, 1, 2, 3) if j > 1 else (2, 3))
             if ahead < n_tiles:
-                quantize_x(ahead, 1)
+                quantize_x(ahead, both)
                 multiply(ahead)
-            if j == n_tiles - 1:
-                store_scales(0, (B - 1) * S)
-        store_scales((B - 1) * S, B * S)
+            if done >= 1:
+                quantize_y(done - 1)
+                if done - 1 in SCALE_STORES:
+                    upto = (TILES[done - 1][-1] + 1) * S
+                    store_scales(stored, upto, [nc.sync] * 4)
+                    stored = upto
+            round_y(done)
+        quantize_y(n_tiles - 1)
+        store_scales(stored, B * S, [nc.sync, nc.sync, nc.scalar, nc.scalar])

@@ -18,13 +18,14 @@ P = 128
 PACK = 4
 K_PASS = P * PACK
 PASSES = C // K_PASS
-RUN = 4
+RUN = 2
 TILES = [[0]] + [[b, b + 1] for b in range(1, B - 1, 2)] + [[B - 1]]
 LEAD = 2
 SCALAR_UNITS = [(b, 0) for b in (1, 2, 3, 5, 7, 9, 11, 13)]
 PAIR = 2
 SCALAR_SAMPLES = {len(TILES) - 2: 64, len(TILES) - 1: 96}
 SCALE_STORES = (2, 5)
+HALF_STORES_FROM = len(TILES) - 3
 
 
 def tile_eeg_log_power_planes_g2_kernel(tc, x, w, power_offset, gain, out_0, out_1, out_2):
@@ -64,8 +65,6 @@ def tile_eeg_log_power_planes_g2_kernel(tc, x, w, power_offset, gain, out_0, out
 
         nc.scalar.dma_start(out=off_bf[:], in_=power_offset.rearrange("(p t) -> p t", t=PACK))
         nc.scalar.dma_start(out=gain_bf[:], in_=gain.rearrange("(p t) -> p t", t=PACK))
-        nc.scalar.copy(out=off[:], in_=off_bf[:])
-        nc.scalar.copy(out=gn[:], in_=gain_bf[:])
         for g in range(PASSES):
             load_w(g)
             nc.sync.dma_start(out=x_raw[0][:, g], in_=x_view(0)[:, g])
@@ -150,6 +149,9 @@ def tile_eeg_log_power_planes_g2_kernel(tc, x, w, power_offset, gain, out_0, out
             nb = len(TILES[i])
             if ts[0] == 0:
                 ys[i] = y_pool.tile([P, 2, PACK, S], F32, name="y")
+            b0 = TILES[i][0]
+            y_hbm = out_0[b0 : b0 + nb].rearrange("b (p t) s -> p b t s", t=PACK)
+            per_store = PAIR if i >= HALF_STORES_FROM else PACK
             for t in ts:
                 nc.vector.tensor_scalar(
                     out=ys[i][:, :nb, t, :],
@@ -158,11 +160,9 @@ def tile_eeg_log_power_planes_g2_kernel(tc, x, w, power_offset, gain, out_0, out
                     scalar2=None,
                     op0=ALU.mult,
                 )
-            if ts[-1] == PACK - 1:
-                b0 = TILES[i][0]
-                nc.sync.dma_start(
-                    out=out_0[b0 : b0 + nb].rearrange("b (p t) s -> p b t s", t=PACK), in_=ys[i][:, :nb]
-                )
+                if (t + 1) % per_store == 0:
+                    slots = slice(t + 1 - per_store, t + 1)
+                    nc.sync.dma_start(out=y_hbm[:, :, slots], in_=ys[i][:, :nb, slots])
 
         def round_y(i):
             nb = len(TILES[i])
@@ -203,6 +203,8 @@ def tile_eeg_log_power_planes_g2_kernel(tc, x, w, power_offset, gain, out_0, out
         open_x(0)
         interleave_w(0, 0, False)
         interleave_w(0, 1, True)
+        nc.scalar.copy(out=off[:], in_=off_bf[:])
+        nc.scalar.copy(out=gn[:], in_=gain_bf[:])
         interleave_x(0, 0, slice(0, 1), False)
         quantize_w(0)
         interleave_w(1, 0, False)

@@ -21,11 +21,11 @@ PASSES = C // K_PASS
 RUN = 2
 TILES = [[0]] + [[b, b + 1] for b in range(1, B - 1, 2)] + [[B - 1]]
 LEAD = 2
-SCALAR_UNITS = [(b, 0) for b in (1, 2, 3, 5, 7, 9, 11, 13)]
+SCALAR_UNITS = [(b, 0) for b in (1, 2, 5, 9, 13)]
 PAIR = 2
-SCALAR_SAMPLES = {len(TILES) - 2: 64, len(TILES) - 1: 96}
-SCALE_STORES = (2, 5)
-HALF_STORES_FROM = len(TILES) - 3
+SCALAR_SAMPLES = {len(TILES) - 3: S, len(TILES) - 2: 64, len(TILES) - 1: S}
+CAST_LAG = 2
+SCALE_STORES = (2, 4)
 
 
 def tile_eeg_log_power_planes_g2_kernel(tc, x, w, power_offset, gain, out_0, out_1, out_2):
@@ -40,8 +40,8 @@ def tile_eeg_log_power_planes_g2_kernel(tc, x, w, power_offset, gain, out_0, out
         xq_pool = ctx.enter_context(tc.tile_pool(name="xq", bufs=4))
         sq_pool = ctx.enter_context(tc.tile_pool(name="sq", bufs=4))
         lg_pool = ctx.enter_context(tc.tile_pool(name="lg", bufs=8))
-        y_pool = ctx.enter_context(tc.tile_pool(name="y", bufs=6))
-        yb_pool = ctx.enter_context(tc.tile_pool(name="yb", bufs=2))
+        y_pool = ctx.enter_context(tc.tile_pool(name="y", bufs=5))
+        yb_pool = ctx.enter_context(tc.tile_pool(name="yb", bufs=3))
         psum = ctx.enter_context(tc.psum_pool(name="psum", bufs=8))
         ctx.enter_context(tc.manual_schedule())
 
@@ -151,7 +151,7 @@ def tile_eeg_log_power_planes_g2_kernel(tc, x, w, power_offset, gain, out_0, out
                 ys[i] = y_pool.tile([P, 2, PACK, S], F32, name="y")
             b0 = TILES[i][0]
             y_hbm = out_0[b0 : b0 + nb].rearrange("b (p t) s -> p b t s", t=PACK)
-            per_store = PAIR if i >= HALF_STORES_FROM else PACK
+            per_store = PACK
             for t in ts:
                 nc.vector.tensor_scalar(
                     out=ys[i][:, :nb, t, :],
@@ -170,7 +170,8 @@ def tile_eeg_log_power_planes_g2_kernel(tc, x, w, power_offset, gain, out_0, out
             dst = ybs[i][:, : nb * S * PACK].rearrange("p (b c r t) -> p b c t r", b=nb, r=PAIR, t=PACK)
             src = ys[i][:, :nb].rearrange("p b t (c r) -> p b c t r", r=PAIR)
             cut = (S - SCALAR_SAMPLES.get(i, 0)) // PAIR
-            nc.vector.tensor_copy(out=dst[:, :, :cut], in_=src[:, :, :cut])
+            if cut > 0:
+                nc.vector.tensor_copy(out=dst[:, :, :cut], in_=src[:, :, :cut])
             if i in SCALAR_SAMPLES:
                 nc.scalar.copy(out=dst[:, :, cut:], in_=src[:, :, cut:])
 
@@ -178,7 +179,9 @@ def tile_eeg_log_power_planes_g2_kernel(tc, x, w, power_offset, gain, out_0, out
             n = width(i)
             cols = slice(TILES[i][0] * S, TILES[i][0] * S + n)
             nc.vector.quantize_mx(out=y_words[:, cols].bitcast(FP8X4), scales=y_scales[:, cols], in_=ybs[i][:, : n * PACK])
-            nc.sync.dma_start(out=words_hbm[:, cols], in_=y_words[:, cols].bitcast(I32))
+
+        def store_words(first, last):
+            nc.sync.dma_start(out=words_hbm[:, first:last], in_=y_words[:, first:last].bitcast(I32))
 
         def store_scales(first, last, queues):
             cols = slice(first // PACK, last // PACK)
@@ -257,16 +260,25 @@ def tile_eeg_log_power_planes_g2_kernel(tc, x, w, power_offset, gain, out_0, out
             if ahead < n_tiles:
                 for b, gs in vector_units(ahead):
                     interleave_x(ahead, b, gs, False)
-            apply_gain(done, (0, 1, 2, 3) if j > 1 else (2, 3))
+            cast = done - CAST_LAG
+            if j > 1:
+                apply_gain(done, (0, 1))
+            if cast >= 1:
+                quantize_y(cast - 1)
+                upto = (TILES[cast - 1][-1] + 1) * S
+                store_words(TILES[cast - 1][0] * S, upto)
+                if cast - 1 in SCALE_STORES:
+                    store_scales(stored, upto, [nc.sync] * 4)
+                    stored = upto
+            apply_gain(done, (2, 3))
             if ahead < n_tiles:
                 quantize_x(ahead, both)
                 multiply(ahead)
-            if done >= 1:
-                quantize_y(done - 1)
-                if done - 1 in SCALE_STORES:
-                    upto = (TILES[done - 1][-1] + 1) * S
-                    store_scales(stored, upto, [nc.sync] * 4)
-                    stored = upto
-            round_y(done)
-        quantize_y(n_tiles - 1)
-        store_scales(stored, B * S, [nc.sync, nc.sync, nc.scalar, nc.scalar])
+            if cast >= 0:
+                round_y(cast)
+        for i in range(n_tiles - CAST_LAG, n_tiles):
+            round_y(i)
+        for i in range(n_tiles - CAST_LAG - 1, n_tiles):
+            quantize_y(i)
+            store_words(TILES[i][0] * S, (TILES[i][-1] + 1) * S)
+        store_scales(stored, B * S, [nc.sync] * 4)

from contextlib import ExitStack

import concourse.mybir as mybir

B, C, S, F = 16, 1024, 256, 512
FLOPS = 2 * B * C * S * F

F32 = mybir.dt.float32
BF16 = mybir.dt.bfloat16
I32 = mybir.dt.int32
U32 = mybir.dt.uint32
U8 = mybir.dt.uint8
FP8X4 = mybir.dt.float8_e4m3fn_x4
ACT = mybir.ActivationFunctionType
ALU = mybir.AluOpType

P = 128
PACK = 4
K_PASS = P * PACK
PASSES = C // K_PASS
RUN = 2
TILES = [[0]] + [[b, b + 1] for b in range(1, B - 1, 2)] + [[B - 1]]
LEAD = 2
SCALAR_UNITS = [(b, 0) for b in (1, 2, 5, 9, 13)]
PAIR = 2
SCALAR_SAMPLES = {len(TILES) - 3: S, len(TILES) - 2: 64, len(TILES) - 1: S}
CAST_LAG = 2
SCALE_STORES = (2, 4)


def tile_eeg_log_power_planes_g2_kernel(tc, x, w, power_offset, gain, out_0, out_1, out_2):
    nc = tc.nc
    n_tiles = len(TILES)
    words_hbm = out_1[0].rearrange("p m t -> p (m t)").bitcast(I32)
    scales_hbm = out_2[0].bitcast(I32)

    with ExitStack() as ctx:
        keep = ctx.enter_context(tc.tile_pool(name="keep", bufs=1))
        xg_pool = ctx.enter_context(tc.tile_pool(name="xg", bufs=3))
        xq_pool = ctx.enter_context(tc.tile_pool(name="xq", bufs=4))
        sq_pool = ctx.enter_context(tc.tile_pool(name="sq", bufs=4))
        lg_pool = ctx.enter_context(tc.tile_pool(name="lg", bufs=8))
        y_pool = ctx.enter_context(tc.tile_pool(name="y", bufs=5))
        yb_pool = ctx.enter_context(tc.tile_pool(name="yb", bufs=3))
        psum = ctx.enter_context(tc.psum_pool(name="psum", bufs=8))
        ctx.enter_context(tc.manual_schedule())

        off_bf = keep.tile([P, PACK], BF16, name="off_bf")
        gain_bf = keep.tile([P, PACK], BF16, name="gain_bf")
        off = keep.tile([P, PACK], F32, name="off")
        gn = keep.tile([P, PACK], F32, name="gn")
        w_raw = [keep.tile([P, PACK, F], BF16, name="w_raw%d" % g) for g in range(PASSES)]
        w_grouped = [keep.tile([P, F * PACK], BF16, name="w_grouped%d" % g, align_bytes=64) for g in range(PASSES)]
        w_codes = [keep.tile([P, F], U32, name="w_codes%d" % g, align_bytes=64) for g in range(PASSES)]
        w_scales = [keep.tile([P, F], U8, name="w_scales%d" % g, align_bytes=64) for g in range(PASSES)]
        x_raw = [keep.tile([P, PASSES, PACK, S], BF16, name="x_raw%d" % b) for b in range(B)]
        y_words = keep.tile([P, B * S], U32, name="y_words", align_bytes=64)
        y_scales = keep.tile([P, B * S], U8, name="y_scales", align_bytes=64)

        def load_w(g):
            nc.sync.dma_start(out=w_raw[g][:], in_=w[g * K_PASS : (g + 1) * K_PASS, :].rearrange("(p j) f -> p j f", j=PACK))

        def x_view(b):
            return x[b].rearrange("(g p j) s -> p g j s", g=PASSES, j=PACK)

        nc.scalar.dma_start(out=off_bf[:], in_=power_offset.rearrange("(p t) -> p t", t=PACK))
        nc.scalar.dma_start(out=gain_bf[:], in_=gain.rearrange("(p t) -> p t", t=PACK))
        for g in range(PASSES):
            load_w(g)
            nc.sync.dma_start(out=x_raw[0][:, g], in_=x_view(0)[:, g])
        for b in range(1, B):
            nc.sync.dma_start(out=x_raw[b][:], in_=x_view(b))

        x_grouped, x_codes, x_scales, banks, squares, logs, ys, ybs = {}, {}, {}, {}, {}, {}, {}, {}

        def width(i):
            return len(TILES[i]) * S

        def copy_on(on_scalar, out, in_):
            if on_scalar:
                nc.scalar.copy(out=out, in_=in_)
            else:
                nc.vector.tensor_copy(out=out, in_=in_)

        def interleave_w(g, half, on_scalar):
            ms = slice(32 * half, 32 * half + 32)
            dst = w_grouped[g][:].rearrange("p (t m e j) -> p m t j e", t=PACK, e=PAIR, j=PACK)[:, ms]
            src = w_raw[g][:].rearrange("p j (m e t) -> p m t j e", t=PACK, e=PAIR)[:, ms]
            copy_on(on_scalar, dst, src)

        def quantize_w(g):
            nc.vector.quantize_mx(out=w_codes[g][:].bitcast(FP8X4), scales=w_scales[g][:], in_=w_grouped[g][:])

        def open_x(i):
            x_grouped[i] = xg_pool.tile([P, PASSES * 2 * S * PACK], BF16, name="x_grouped", align_bytes=64)
            x_codes[i] = xq_pool.tile([P, PASSES * 2 * S], U32, name="x_codes", align_bytes=64)
            x_scales[i] = xq_pool.tile([P, PASSES * 2 * S], U8, name="x_scales", align_bytes=64)

        def interleave_x(i, b, gs, on_scalar):
            at = TILES[i].index(b) * S * PACK
            by_pass = x_grouped[i][:, : PASSES * width(i) * PACK].rearrange("p (g e) -> p g e", g=PASSES)
            dst = by_pass[:, gs, at : at + S * PACK].rearrange("p g (c r j) -> p g c j r", r=RUN, j=PACK)
            src = x_raw[b][:, gs].rearrange("p g j (c r) -> p g c j r", r=RUN)
            copy_on(on_scalar, dst, src)

        def quantize_x(i, gs):
            n = width(i)
            cols = slice(gs.start * n, gs.stop * n)
            nc.vector.quantize_mx(
                out=x_codes[i][:, cols].bitcast(FP8X4),
                scales=x_scales[i][:, cols],
                in_=x_grouped[i][:, cols.start * PACK : cols.stop * PACK],
            )

        def multiply(i):
            n = width(i)
            per_bank = 2 * S // n
            for t in range(PACK):
                if t % per_bank == 0:
                    bank = psum.tile([P, 2 * S], F32, name="bank")
                    banks[i, t // per_bank] = bank
                at = (t % per_bank) * n
                cols = slice(t * P, (t + 1) * P)
                for g in range(PASSES):
                    nc.tensor.matmul_mx(
                        out=bank[:, at : at + n],
                        lhsT=w_codes[g][:, cols].bitcast(FP8X4),
                        lhsT_scale=w_scales[g][:, cols],
                        rhs=x_codes[i][:, g * n : (g + 1) * n].bitcast(FP8X4),
                        rhs_scale=x_scales[i][:, g * n : (g + 1) * n],
                        start=(g == 0),
                        stop=(g == PASSES - 1),
                    )

        def square(i, k):
            squares[i, k] = sq_pool.tile([P, 2 * S], F32, name="square")
            nc.scalar.activation(out=squares[i, k][:], in_=banks[i, k][:], func=ACT.Square)

        def log(i, t):
            n = width(i)
            per_bank = 2 * S // n
            at = (t % per_bank) * n
            logs[i, t] = lg_pool.tile([P, 2 * S], F32, name="logp")
            nc.scalar.activation(
                out=logs[i, t][:, :n], in_=squares[i, t // per_bank][:, at : at + n], func=ACT.Ln, bias=off[:, t : t + 1]
            )

        def apply_gain(i, ts):
            nb = len(TILES[i])
            if ts[0] == 0:
                ys[i] = y_pool.tile([P, 2, PACK, S], F32, name="y")
            b0 = TILES[i][0]
            y_hbm = out_0[b0 : b0 + nb].rearrange("b (p t) s -> p b t s", t=PACK)
            per_store = PACK
            for t in ts:
                nc.vector.tensor_scalar(
                    out=ys[i][:, :nb, t, :],
                    in0=logs[i, t][:, : nb * S].rearrange("p (b s) -> p b s", s=S),
                    scalar1=gn[:, t : t + 1],
                    scalar2=None,
                    op0=ALU.mult,
                )
                if (t + 1) % per_store == 0:
                    slots = slice(t + 1 - per_store, t + 1)
                    nc.sync.dma_start(out=y_hbm[:, :, slots], in_=ys[i][:, :nb, slots])

        def round_y(i):
            nb = len(TILES[i])
            ybs[i] = yb_pool.tile([P, 2 * S * PACK], BF16, name="y_bf", align_bytes=64)
            dst = ybs[i][:, : nb * S * PACK].rearrange("p (b c r t) -> p b c t r", b=nb, r=PAIR, t=PACK)
            src = ys[i][:, :nb].rearrange("p b t (c r) -> p b c t r", r=PAIR)
            cut = (S - SCALAR_SAMPLES.get(i, 0)) // PAIR
            if cut > 0:
                nc.vector.tensor_copy(out=dst[:, :, :cut], in_=src[:, :, :cut])
            if i in SCALAR_SAMPLES:
                nc.scalar.copy(out=dst[:, :, cut:], in_=src[:, :, cut:])

        def quantize_y(i):
            n = width(i)
            cols = slice(TILES[i][0] * S, TILES[i][0] * S + n)
            nc.vector.quantize_mx(out=y_words[:, cols].bitcast(FP8X4), scales=y_scales[:, cols], in_=ybs[i][:, : n * PACK])

        def store_words(first, last):
            nc.sync.dma_start(out=words_hbm[:, first:last], in_=y_words[:, first:last].bitcast(I32))

        def store_scales(first, last, queues):
            cols = slice(first // PACK, last // PACK)
            for q in range(4):
                queues[q].dma_start(
                    out=scales_hbm[4 * q : 4 * q + 4, cols], in_=y_scales[:].bitcast(I32)[32 * q : 32 * q + 4, cols]
                )

        def vector_units(i):
            units = []
            for b in TILES[i]:
                first = 1 if (b, 0) in SCALAR_UNITS else 0
                units.append((b, slice(first, PASSES)))
            return units

        def scalar_interleaves(i):
            for b in TILES[i]:
                if (b, 0) in SCALAR_UNITS:
                    interleave_x(i, b, slice(0, 1), True)

        both = slice(0, PASSES)
        open_x(0)
        interleave_w(0, 0, False)
        interleave_w(0, 1, True)
        nc.scalar.copy(out=off[:], in_=off_bf[:])
        nc.scalar.copy(out=gn[:], in_=gain_bf[:])
        interleave_x(0, 0, slice(0, 1), False)
        quantize_w(0)
        interleave_w(1, 0, False)
        interleave_w(1, 1, True)
        quantize_x(0, slice(0, 1))
        interleave_x(0, 0, slice(1, 2), False)
        quantize_w(1)
        quantize_x(0, slice(1, 2))
        multiply(0)
        open_x(1)
        scalar_interleaves(1)
        for b, gs in vector_units(1):
            interleave_x(1, b, gs, False)

        open_x(2)
        square(0, 0)
        square(0, 1)
        scalar_interleaves(2)
        for t in range(PACK):
            log(0, t)
        units = vector_units(2)
        interleave_x(2, units[0][0], units[0][1], False)
        quantize_x(1, both)
        multiply(1)
        interleave_x(2, units[1][0], units[1][1], False)

        stored = 0
        for j in range(1, n_tiles + 1):
            ahead = j + LEAD
            done = j - 1
            if ahead < n_tiles:
                open_x(ahead)
                scalar_interleaves(ahead)
            if j < n_tiles:
                if len(TILES[j]) == 2:
                    for pair in ((0, 1), (2, 3)):
                        for t in pair:
                            square(j, t)
                        for t in pair:
                            log(j, t)
                else:
                    square(j, 0)
                    square(j, 1)
                    for t in range(PACK):
                        log(j, t)
            if j == 1:
                apply_gain(done, (0, 1))
                quantize_x(2, both)
                multiply(2)
            if ahead < n_tiles:
                for b, gs in vector_units(ahead):
                    interleave_x(ahead, b, gs, False)
            cast = done - CAST_LAG
            if j > 1:
                apply_gain(done, (0, 1))
            if cast >= 1:
                quantize_y(cast - 1)
                upto = (TILES[cast - 1][-1] + 1) * S
                store_words(TILES[cast - 1][0] * S, upto)
                if cast - 1 in SCALE_STORES:
                    store_scales(stored, upto, [nc.sync] * 4)
                    stored = upto
            apply_gain(done, (2, 3))
            if ahead < n_tiles:
                quantize_x(ahead, both)
                multiply(ahead)
            if cast >= 0:
                round_y(cast)
        for i in range(n_tiles - CAST_LAG, n_tiles):
            round_y(i)
        for i in range(n_tiles - CAST_LAG - 1, n_tiles):
            quantize_y(i)
            store_words(TILES[i][0] * S, (TILES[i][-1] + 1) * S)
        store_scales(stored, B * S, [nc.sync] * 4)
